import numpy as np
import ml_dtypes

BF16 = ml_dtypes.bfloat16


def bf(x):
    return np.asarray(x, np.float32).astype(BF16)


def f32(x):
    return np.asarray(x, np.float32)


def f64(x):
    return np.asarray(x).astype(np.float64)


def striped(idx):
    return np.tile(idx.reshape(-1, 16).T, (8, 1))


def rows(idx, k):
    return np.tile(idx, (k, 1))


def look(tab, idx):
    return np.take_along_axis(f64(tab), rows(idx, len(tab)), axis=1)


K, S, V, N, M = 256, 2048, 2048, 2048, 512


def silu(v):
    return v / (1.0 + np.exp(-v))


def setup_inputs():
    return {"tab": f32(np.random.standard_normal((2, K, S))), "y": f32(np.random.standard_normal((K, V))), "w": bf(np.random.standard_normal((K, M)) / np.sqrt(K)), "b": f32(0.5 * np.random.standard_normal((M, 1))), "offs": striped(np.random.permutation(S)[:N])}


def reference(tab, y, w, b, offs):
    idx = offs[:16].T.reshape(-1)
    x = (np.minimum(look(tab[0], idx), f64(y))) * (silu(look(tab[1], idx)))
    return np.maximum(f64(w).T @ x + f64(b), 0.0)

@@ -1,0 +1,80 @@
+import concourse.mybir as mybir
+
+F32, BF16, U16 = mybir.dt.float32, mybir.dt.bfloat16, mybir.dt.uint16
+MIN, MULT, ADD, MAX = mybir.AluOpType.min, mybir.AluOpType.mult, mybir.AluOpType.add, mybir.AluOpType.max
+SILU, RELU = mybir.ActivationFunctionType.Silu, mybir.ActivationFunctionType.Relu
+
+P = 128
+R = 256
+S = 2048
+N = 2048
+M = 512
+CHUNK = 512
+PER_COLUMN = 16
+
+R_BLOCKS, M_BLOCKS, CHUNKS = R // P, M // P, N // CHUNK
+
+FLOPS = 2 * R * M * N
+
+
+def tile_lookup_vg_minsilu_relu_kernel(tc, tab, y, w, b, offs, out):
+    nc = tc.nc
+    with (
+        tc.tile_pool(name="held", bufs=1) as held,
+        tc.psum_pool(name="psum", bufs=8) as psum,
+    ):
+        offsets = held.tile([P, N // PER_COLUMN], U16, name="offsets")
+        nc.sync.dma_start(offsets[:], offs)
+
+        values = [held.tile([P, S], F32, name=f"values{r}") for r in range(R_BLOCKS)]
+        gates = [held.tile([P, S], F32, name=f"gates{r}") for r in range(R_BLOCKS)]
+        weights = [held.tile([P, M], BF16, name=f"weights{r}") for r in range(R_BLOCKS)]
+        bias = held.tile([P, M_BLOCKS], F32, name="bias")
+        stream = [[held.tile([P, CHUNK], F32, name=f"stream{r}_{c}") for c in range(CHUNKS)] for r in range(R_BLOCKS)]
+
+        for r in range(R_BLOCKS):
+            rows = slice(r * P, (r + 1) * P)
+            nc.gpsimd.dma_start(weights[r][:], w[rows, :])
+        nc.gpsimd.dma_start(bias[:], b.rearrange("(m p) one -> p (m one)", p=P))
+        for r in range(R_BLOCKS):
+            rows = slice(r * P, (r + 1) * P)
+            nc.sync.dma_start(values[r][:], tab[0, rows, :])
+            for c in range(CHUNKS):
+                nc.sync.dma_start(stream[r][c][:], y[rows, c * CHUNK : (c + 1) * CHUNK])
+            nc.sync.dma_start(gates[r][:], tab[1, rows, :])
+
+        def chunk_of_list(c):
+            per_chunk = CHUNK // PER_COLUMN
+            return offsets[:, c * per_chunk : (c + 1) * per_chunk]
+
+        def product(r, c):
+            lowest = held.tile([P, CHUNK], F32, name=f"lowest{r}_{c}")
+            nc.vector.tensor_tensor(lowest[:], values[r][:].indirect(chunk_of_list(c)), stream[r][c][:], MIN)
+            opened = held.tile([P, CHUNK], F32, name=f"opened{r}_{c}")
+            nc.scalar.activation(opened[:], gates[r][:].indirect(chunk_of_list(c)), SILU)
+            x = held.tile([P, CHUNK], BF16, name=f"x{r}_{c}")
+            nc.vector.tensor_tensor(x[:], lowest[:], opened[:], MULT)
+            return x
+
+        xs = {}
+        for r in range(R_BLOCKS):
+            for c in range(CHUNKS):
+                xs[r, c] = product(r, c)
+
+        for c in range(CHUNKS):
+            for m in range(M_BLOCKS):
+                bank = psum.tile([P, CHUNK], F32, name="bank")
+                for r in range(R_BLOCKS):
+                    nc.tensor.matmul(
+                        bank[:],
+                        weights[r][:, m * P : (m + 1) * P],
+                        xs[r, c][:],
+                        start=r == 0,
+                        stop=r == R_BLOCKS - 1,
+                    )
+                result = held.tile([P, CHUNK], F32, name=f"result{c}_{m}")
+                if m % 2 == 0:
+                    nc.scalar.activation(result[:], bank[:], RELU, bias=bias[:, m : m + 1])
+                else:
+                    nc.vector.tensor_scalar(result[:], bank[:], bias[:, m : m + 1], 0.0, ADD, MAX)
+                nc.sync.dma_start(out[m * P : (m + 1) * P, c * CHUNK : (c + 1) * CHUNK], result[:])

@@ -32,49 +32,74 @@ def tile_lookup_vg_minsilu_relu_kernel(tc, tab, y, w, b, offs, out):
         bias = held.tile([P, M_BLOCKS], F32, name="bias")
         stream = [[held.tile([P, CHUNK], F32, name=f"stream{r}_{c}") for c in range(CHUNKS)] for r in range(R_BLOCKS)]
 
+        def load_stream(r, c):
+            nc.sync.dma_start(stream[r][c][:], y[r * P : (r + 1) * P, c * CHUNK : (c + 1) * CHUNK])
+
+        warm = held.tile([P, 1], F32, name="warm")
+        nc.vector.memset(warm[:], 0.0)
+        warm_out = held.tile([P, 1], F32, name="warm_out")
+        nc.scalar.activation(warm_out[:], warm[:], SILU)
+
+        nc.scalar.dma_start(bias[:], b.rearrange("(m p) one -> p (m one)", p=P))
+        nc.sync.dma_start(values[0][:], tab[0, 0:P, :])
+        load_stream(0, 0)
+        load_stream(0, 1)
+        nc.sync.dma_start(gates[0][:], tab[1, 0:P, :])
+        load_stream(0, 2)
+        load_stream(0, 3)
+        nc.sync.dma_start(values[1][:], tab[0, P : 2 * P, :])
+        load_stream(1, 0)
+        nc.sync.dma_start(gates[1][:], tab[1, P : 2 * P, :])
         for r in range(R_BLOCKS):
-            rows = slice(r * P, (r + 1) * P)
-            nc.gpsimd.dma_start(weights[r][:], w[rows, :])
-        nc.gpsimd.dma_start(bias[:], b.rearrange("(m p) one -> p (m one)", p=P))
-        for r in range(R_BLOCKS):
-            rows = slice(r * P, (r + 1) * P)
-            nc.sync.dma_start(values[r][:], tab[0, rows, :])
-            for c in range(CHUNKS):
-                nc.sync.dma_start(stream[r][c][:], y[rows, c * CHUNK : (c + 1) * CHUNK])
-            nc.sync.dma_start(gates[r][:], tab[1, rows, :])
+            nc.sync.dma_start(weights[r][:], w[r * P : (r + 1) * P, :])
+        for c in range(1, CHUNKS):
+            load_stream(1, c)
 
         def chunk_of_list(c):
             per_chunk = CHUNK // PER_COLUMN
             return offsets[:, c * per_chunk : (c + 1) * per_chunk]
 
-        def product(r, c):
+        def lowest_values(r, c):
             lowest = held.tile([P, CHUNK], F32, name=f"lowest{r}_{c}")
             nc.vector.tensor_tensor(lowest[:], values[r][:].indirect(chunk_of_list(c)), stream[r][c][:], MIN)
+            return lowest
+
+        def opened_gates(r, c):
             opened = held.tile([P, CHUNK], F32, name=f"opened{r}_{c}")
             nc.scalar.activation(opened[:], gates[r][:].indirect(chunk_of_list(c)), SILU)
+            return opened
+
+        def product(r, c, lowest, opened):
             x = held.tile([P, CHUNK], BF16, name=f"x{r}_{c}")
             nc.vector.tensor_tensor(x[:], lowest[:], opened[:], MULT)
             return x
 
-        xs = {}
-        for r in range(R_BLOCKS):
-            for c in range(CHUNKS):
-                xs[r, c] = product(r, c)
-
-        for c in range(CHUNKS):
-            for m in range(M_BLOCKS):
-                bank = psum.tile([P, CHUNK], F32, name="bank")
-                for r in range(R_BLOCKS):
+        def layer(c, xs):
+            banks = [psum.tile([P, CHUNK], F32, name="bank") for m in range(M_BLOCKS)]
+            for r in range(R_BLOCKS):
+                for m in range(M_BLOCKS):
                     nc.tensor.matmul(
-                        bank[:],
+                        banks[m][:],
                         weights[r][:, m * P : (m + 1) * P],
-                        xs[r, c][:],
+                        xs[r][:],
                         start=r == 0,
                         stop=r == R_BLOCKS - 1,
                     )
+            for m in range(M_BLOCKS):
                 result = held.tile([P, CHUNK], F32, name=f"result{c}_{m}")
-                if m % 2 == 0:
-                    nc.scalar.activation(result[:], bank[:], RELU, bias=bias[:, m : m + 1])
+                if m < M_BLOCKS - 1:
+                    nc.scalar.activation(result[:], banks[m][:], RELU, bias=bias[:, m : m + 1])
                 else:
-                    nc.vector.tensor_scalar(result[:], bank[:], bias[:, m : m + 1], 0.0, ADD, MAX)
+                    nc.vector.tensor_scalar(result[:], banks[m][:], bias[:, m : m + 1], 0.0, ADD, MAX)
                 nc.sync.dma_start(out[m * P : (m + 1) * P, c * CHUNK : (c + 1) * CHUNK], result[:])
+
+        lowest = [lowest_values(0, c) for c in range(CHUNKS)]
+        opened = [opened_gates(0, c) for c in range(CHUNKS)]
+        first = [product(0, c, lowest[c], opened[c]) for c in range(CHUNKS)]
+
+        second = []
+        for c in range(CHUNKS):
+            second.append(product(1, c, lowest_values(1, c), opened_gates(1, c)))
+            if c > 0:
+                layer(c - 1, [first[c - 1], second[c - 1]])
+        layer(CHUNKS - 1, [first[CHUNKS - 1], second[CHUNKS - 1]])

@@ -40,7 +40,6 @@ def tile_lookup_vg_minsilu_relu_kernel(tc, tab, y, w, b, offs, out):
         warm_out = held.tile([P, 1], F32, name="warm_out")
         nc.scalar.activation(warm_out[:], warm[:], SILU)
 
-        nc.scalar.dma_start(bias[:], b.rearrange("(m p) one -> p (m one)", p=P))
         nc.sync.dma_start(values[0][:], tab[0, 0:P, :])
         load_stream(0, 0)
         load_stream(0, 1)
@@ -52,6 +51,7 @@ def tile_lookup_vg_minsilu_relu_kernel(tc, tab, y, w, b, offs, out):
         nc.sync.dma_start(gates[1][:], tab[1, P : 2 * P, :])
         for r in range(R_BLOCKS):
             nc.sync.dma_start(weights[r][:], w[r * P : (r + 1) * P, :])
+        nc.sync.dma_start(bias[:], b.rearrange("(m p) one -> p (m one)", p=P))
         for c in range(1, CHUNKS):
             load_stream(1, c)
 

@@ -10,9 +10,11 @@ S = 2048
 N = 2048
 M = 512
 CHUNK = 512
-PER_COLUMN = 16
+PSUM_BANKS = 8
+ENTRIES_PER_COLUMN = 16
+OFFSET_COLUMNS = CHUNK // ENTRIES_PER_COLUMN
 
-R_BLOCKS, M_BLOCKS, CHUNKS = R // P, M // P, N // CHUNK
+ROW_BLOCKS, OUT_BLOCKS, CHUNKS = R // P, M // P, N // CHUNK
 
 FLOPS = 2 * R * M * N
 
@@ -21,50 +23,52 @@ def tile_lookup_vg_minsilu_relu_kernel(tc, tab, y, w, b, offs, out):
     nc = tc.nc
     with (
         tc.tile_pool(name="held", bufs=1) as held,
-        tc.psum_pool(name="psum", bufs=8) as psum,
+        tc.tile_pool(name="single", bufs=1) as single,
+        tc.psum_pool(name="psum", bufs=PSUM_BANKS) as psum,
     ):
-        offsets = held.tile([P, N // PER_COLUMN], U16, name="offsets")
+        offsets = held.tile([P, N // ENTRIES_PER_COLUMN], U16, name="offsets")
         nc.sync.dma_start(offsets[:], offs)
 
-        values = [held.tile([P, S], F32, name=f"values{r}") for r in range(R_BLOCKS)]
-        gates = [held.tile([P, S], F32, name=f"gates{r}") for r in range(R_BLOCKS)]
-        weights = [held.tile([P, M], BF16, name=f"weights{r}") for r in range(R_BLOCKS)]
-        bias = held.tile([P, M_BLOCKS], F32, name="bias")
-        stream = [[held.tile([P, CHUNK], F32, name=f"stream{r}_{c}") for c in range(CHUNKS)] for r in range(R_BLOCKS)]
+        values = [held.tile([P, S], F32, name=f"values{r}") for r in range(ROW_BLOCKS)]
+        gates = [held.tile([P, S], F32, name=f"gates{r}") for r in range(ROW_BLOCKS)]
+        stream = [
+            [held.tile([P, CHUNK], F32, name=f"stream{r}_{c}") for c in range(CHUNKS)] for r in range(ROW_BLOCKS)
+        ]
+        weights = [held.tile([P, M], BF16, name=f"weights{r}") for r in range(ROW_BLOCKS)]
+        bias = held.tile([P, OUT_BLOCKS], F32, name="bias")
 
-        def load_stream(r, c):
-            nc.sync.dma_start(stream[r][c][:], y[r * P : (r + 1) * P, c * CHUNK : (c + 1) * CHUNK])
+        def rows(block):
+            return slice(block * P, (block + 1) * P)
 
-        warm = held.tile([P, 1], F32, name="warm")
-        nc.vector.memset(warm[:], 0.0)
+        def load_stream(r, chunks):
+            for c in chunks:
+                nc.sync.dma_start(stream[r][c][:], y[rows(r), c * CHUNK : (c + 1) * CHUNK])
+
+        warm_in = held.tile([P, 1], F32, name="warm_in")
         warm_out = held.tile([P, 1], F32, name="warm_out")
-        nc.scalar.activation(warm_out[:], warm[:], SILU)
+        nc.vector.memset(warm_in[:], 0.0)
+        nc.scalar.activation(warm_out[:], warm_in[:], SILU)
 
-        nc.sync.dma_start(values[0][:], tab[0, 0:P, :])
-        load_stream(0, 0)
-        load_stream(0, 1)
-        nc.sync.dma_start(gates[0][:], tab[1, 0:P, :])
-        load_stream(0, 2)
-        load_stream(0, 3)
-        nc.sync.dma_start(values[1][:], tab[0, P : 2 * P, :])
-        load_stream(1, 0)
-        nc.sync.dma_start(gates[1][:], tab[1, P : 2 * P, :])
-        for r in range(R_BLOCKS):
-            nc.sync.dma_start(weights[r][:], w[r * P : (r + 1) * P, :])
+        first_half, second_half = range(CHUNKS // 2), range(CHUNKS // 2, CHUNKS)
+        nc.sync.dma_start(values[0][:], tab[0, rows(0), :])
+        load_stream(0, first_half)
+        nc.sync.dma_start(gates[0][:], tab[1, rows(0), :])
+        load_stream(0, second_half)
+        nc.sync.dma_start(values[1][:], tab[0, rows(1), :])
+        nc.sync.dma_start(gates[1][:], tab[1, rows(1), :])
+        load_stream(1, range(1))
+        for r in range(ROW_BLOCKS):
+            nc.sync.dma_start(weights[r][:], w[rows(r), :])
+        load_stream(1, range(1, CHUNKS))
         nc.sync.dma_start(bias[:], b.rearrange("(m p) one -> p (m one)", p=P))
-        for c in range(1, CHUNKS):
-            load_stream(1, c)
 
         def chunk_of_list(c):
-            per_chunk = CHUNK // PER_COLUMN
-            return offsets[:, c * per_chunk : (c + 1) * per_chunk]
+            return offsets[:, c * OFFSET_COLUMNS : (c + 1) * OFFSET_COLUMNS]
 
-        def lowest_values(r, c):
-            lowest = held.tile([P, CHUNK], F32, name=f"lowest{r}_{c}")
+        def look_up_values(r, c, lowest):
             nc.vector.tensor_tensor(lowest[:], values[r][:].indirect(chunk_of_list(c)), stream[r][c][:], MIN)
-            return lowest
 
-        def opened_gates(r, c):
+        def look_up_gates(r, c):
             opened = held.tile([P, CHUNK], F32, name=f"opened{r}_{c}")
             nc.scalar.activation(opened[:], gates[r][:].indirect(chunk_of_list(c)), SILU)
             return opened
@@ -75,31 +79,31 @@ def tile_lookup_vg_minsilu_relu_kernel(tc, tab, y, w, b, offs, out):
             return x
 
         def layer(c, xs):
-            banks = [psum.tile([P, CHUNK], F32, name="bank") for m in range(M_BLOCKS)]
-            for r in range(R_BLOCKS):
-                for m in range(M_BLOCKS):
+            banks = [psum.tile([P, CHUNK], F32, name="bank") for m in range(OUT_BLOCKS)]
+            for r in range(ROW_BLOCKS):
+                for m in range(OUT_BLOCKS):
                     nc.tensor.matmul(
-                        banks[m][:],
-                        weights[r][:, m * P : (m + 1) * P],
-                        xs[r][:],
-                        start=r == 0,
-                        stop=r == R_BLOCKS - 1,
+                        banks[m][:], weights[r][:, rows(m)], xs[r][:], start=r == 0, stop=r == ROW_BLOCKS - 1
                     )
-            for m in range(M_BLOCKS):
+            for m in range(OUT_BLOCKS):
                 result = held.tile([P, CHUNK], F32, name=f"result{c}_{m}")
-                if m < M_BLOCKS - 1:
+                if m < OUT_BLOCKS - 1:
                     nc.scalar.activation(result[:], banks[m][:], RELU, bias=bias[:, m : m + 1])
                 else:
                     nc.vector.tensor_scalar(result[:], banks[m][:], bias[:, m : m + 1], 0.0, ADD, MAX)
-                nc.sync.dma_start(out[m * P : (m + 1) * P, c * CHUNK : (c + 1) * CHUNK], result[:])
+                nc.sync.dma_start(out[rows(m), c * CHUNK : (c + 1) * CHUNK], result[:])
 
-        lowest = [lowest_values(0, c) for c in range(CHUNKS)]
-        opened = [opened_gates(0, c) for c in range(CHUNKS)]
-        first = [product(0, c, lowest[c], opened[c]) for c in range(CHUNKS)]
-
-        second = []
+        lowest_first = [held.tile([P, CHUNK], F32, name=f"lowest_first{c}") for c in range(CHUNKS)]
         for c in range(CHUNKS):
-            second.append(product(1, c, lowest_values(1, c), opened_gates(1, c)))
+            look_up_values(0, c, lowest_first[c])
+        opened_first = [look_up_gates(0, c) for c in range(CHUNKS)]
+        x_first = [product(0, c, lowest_first[c], opened_first[c]) for c in range(CHUNKS)]
+
+        x_second = []
+        for c in range(CHUNKS):
+            lowest_second = single.tile([P, CHUNK], F32, name="lowest_second")
+            look_up_values(1, c, lowest_second)
+            x_second.append(product(1, c, lowest_second, look_up_gates(1, c)))
             if c > 0:
-                layer(c - 1, [first[c - 1], second[c - 1]])
-        layer(CHUNKS - 1, [first[CHUNKS - 1], second[CHUNKS - 1]])
+                layer(c - 1, [x_first[c - 1], x_second[c - 1]])
+        layer(CHUNKS - 1, [x_first[CHUNKS - 1], x_second[CHUNKS - 1]])

import concourse.mybir as mybir

F32, BF16, U16 = mybir.dt.float32, mybir.dt.bfloat16, mybir.dt.uint16
MIN, MULT, ADD, MAX = mybir.AluOpType.min, mybir.AluOpType.mult, mybir.AluOpType.add, mybir.AluOpType.max
SILU, RELU = mybir.ActivationFunctionType.Silu, mybir.ActivationFunctionType.Relu

P = 128
R = 256
S = 2048
N = 2048
M = 512
CHUNK = 512
PSUM_BANKS = 8
ENTRIES_PER_COLUMN = 16
OFFSET_COLUMNS = CHUNK // ENTRIES_PER_COLUMN

ROW_BLOCKS, OUT_BLOCKS, CHUNKS = R // P, M // P, N // CHUNK

FLOPS = 2 * R * M * N


def tile_lookup_vg_minsilu_relu_kernel(tc, tab, y, w, b, offs, out):
    nc = tc.nc
    with (
        tc.tile_pool(name="held", bufs=1) as held,
        tc.tile_pool(name="single", bufs=1) as single,
        tc.psum_pool(name="psum", bufs=PSUM_BANKS) as psum,
    ):
        offsets = held.tile([P, N // ENTRIES_PER_COLUMN], U16, name="offsets")
        nc.sync.dma_start(offsets[:], offs)

        values = [held.tile([P, S], F32, name=f"values{r}") for r in range(ROW_BLOCKS)]
        gates = [held.tile([P, S], F32, name=f"gates{r}") for r in range(ROW_BLOCKS)]
        stream = [
            [held.tile([P, CHUNK], F32, name=f"stream{r}_{c}") for c in range(CHUNKS)] for r in range(ROW_BLOCKS)
        ]
        weights = [held.tile([P, M], BF16, name=f"weights{r}") for r in range(ROW_BLOCKS)]
        bias = held.tile([P, OUT_BLOCKS], F32, name="bias")

        def rows(block):
            return slice(block * P, (block + 1) * P)

        def load_stream(r, chunks):
            for c in chunks:
                nc.sync.dma_start(stream[r][c][:], y[rows(r), c * CHUNK : (c + 1) * CHUNK])

        warm_in = held.tile([P, 1], F32, name="warm_in")
        warm_out = held.tile([P, 1], F32, name="warm_out")
        nc.vector.memset(warm_in[:], 0.0)
        nc.scalar.activation(warm_out[:], warm_in[:], SILU)

        first_half, second_half = range(CHUNKS // 2), range(CHUNKS // 2, CHUNKS)
        nc.sync.dma_start(values[0][:], tab[0, rows(0), :])
        load_stream(0, first_half)
        nc.sync.dma_start(gates[0][:], tab[1, rows(0), :])
        load_stream(0, second_half)
        nc.sync.dma_start(values[1][:], tab[0, rows(1), :])
        nc.sync.dma_start(gates[1][:], tab[1, rows(1), :])
        load_stream(1, range(1))
        for r in range(ROW_BLOCKS):
            nc.sync.dma_start(weights[r][:], w[rows(r), :])
        load_stream(1, range(1, CHUNKS))
        nc.sync.dma_start(bias[:], b.rearrange("(m p) one -> p (m one)", p=P))

        def chunk_of_list(c):
            return offsets[:, c * OFFSET_COLUMNS : (c + 1) * OFFSET_COLUMNS]

        def look_up_values(r, c, lowest):
            nc.vector.tensor_tensor(lowest[:], values[r][:].indirect(chunk_of_list(c)), stream[r][c][:], MIN)

        def look_up_gates(r, c):
            opened = held.tile([P, CHUNK], F32, name=f"opened{r}_{c}")
            nc.scalar.activation(opened[:], gates[r][:].indirect(chunk_of_list(c)), SILU)
            return opened

        def product(r, c, lowest, opened):
            x = held.tile([P, CHUNK], BF16, name=f"x{r}_{c}")
            nc.vector.tensor_tensor(x[:], lowest[:], opened[:], MULT)
            return x

        def layer(c, xs):
            banks = [psum.tile([P, CHUNK], F32, name="bank") for m in range(OUT_BLOCKS)]
            for r in range(ROW_BLOCKS):
                for m in range(OUT_BLOCKS):
                    nc.tensor.matmul(
                        banks[m][:], weights[r][:, rows(m)], xs[r][:], start=r == 0, stop=r == ROW_BLOCKS - 1
                    )
            for m in range(OUT_BLOCKS):
                result = held.tile([P, CHUNK], F32, name=f"result{c}_{m}")
                if m < OUT_BLOCKS - 1:
                    nc.scalar.activation(result[:], banks[m][:], RELU, bias=bias[:, m : m + 1])
                else:
                    nc.vector.tensor_scalar(result[:], banks[m][:], bias[:, m : m + 1], 0.0, ADD, MAX)
                nc.sync.dma_start(out[rows(m), c * CHUNK : (c + 1) * CHUNK], result[:])

        lowest_first = [held.tile([P, CHUNK], F32, name=f"lowest_first{c}") for c in range(CHUNKS)]
        for c in range(CHUNKS):
            look_up_values(0, c, lowest_first[c])
        opened_first = [look_up_gates(0, c) for c in range(CHUNKS)]
        x_first = [product(0, c, lowest_first[c], opened_first[c]) for c in range(CHUNKS)]

        x_second = []
        for c in range(CHUNKS):
            lowest_second = single.tile([P, CHUNK], F32, name="lowest_second")
            look_up_values(1, c, lowest_second)
            x_second.append(product(1, c, lowest_second, look_up_gates(1, c)))
            if c > 0:
                layer(c - 1, [x_first[c - 1], x_second[c - 1]])
        layer(CHUNKS - 1, [x_first[CHUNKS - 1], x_second[CHUNKS - 1]])
